import numpy as np
import ml_dtypes


def mxq(x, axis, fmt="e4m3"):
    dtype, down = {"e4m3": (ml_dtypes.float8_e4m3fn, 7), "e5m2": (ml_dtypes.float8_e5m2, 14)}[fmt]
    v = np.moveaxis(np.asarray(x, np.float32).astype(ml_dtypes.bfloat16).astype(np.float64), axis, -1)
    blocks = v.reshape(v.shape[:-1] + (-1, 32))
    amax = np.abs(blocks).max(-1, keepdims=True)
    byte = np.maximum(np.where(amax > 0, np.frexp(amax)[1] - 1 + 127, 0) - down, 1)
    scale = np.exp2(byte - 127.0)
    codes = (blocks / scale).astype(np.float32).astype(dtype).astype(np.float64)
    return np.moveaxis((codes * scale).reshape(v.shape), -1, axis)


WIDE = False


def mx_kscale(k):
    if not WIDE:
        return np.ones(k)
    levels = np.array([10, -10, 5, -5, 0])
    if k % 512:
        return np.exp2(np.random.permutation(np.resize(levels, k // 32))).repeat(32)
    a = np.empty((k // 512, 16))
    for p in range(k // 512):
        a[p, :8] = np.random.permutation(np.resize(levels, 8))
        for g in range(8):
            far = levels[np.abs(levels - a[p, g]) >= 10]
            a[p, g + 8] = far[np.random.randint(len(far))]
    return np.exp2(a.ravel()).repeat(32)


def f64(x):
    return np.asarray(x).astype(np.float64)


def striped8(idx):
    return np.asarray(idx).reshape(8, -1, 16).transpose(0, 2, 1).reshape(128, -1).astype(np.uint16)


def unstriped8(offs):
    return offs.reshape(8, 16, -1).transpose(0, 2, 1).reshape(8, -1).astype(np.int64)


def pick8(x, idx, run):
    r = np.arange(len(x))
    return x[r[:, None], idx[r % (8 * run) // run]]


def sigmoid(v):
    return 1.0 / (1.0 + np.exp(-v))


D, T, I, Q, X, E, G = 512, 1024, 512, 256, 32, 512, 64


def setup_inputs():
    n = np.random.standard_normal
    idx = np.stack([(np.random.permutation(T // 8)[:I // 8, None] * 8 + np.arange(8)).reshape(-1) for _ in range(8)])
    fd = mx_kscale(D)
    fi = mx_kscale(I)
    ti = np.ones((8, T))
    np.put_along_axis(ti, idx, np.tile(fi, (8, 1)), axis=1)
    return {
        "query": (n((D, Q)) * (np.arange(D)[:, None] // 64 == np.arange(Q) % 8) * 0.0625 * fd[:, None]).astype(np.float32),
        "keys": (n((D, T)) / fd[:, None]).astype(np.float32),
        "th": (np.random.uniform(-0.5, 0.5, (Q, 1))).astype(np.float32),
        "size": (np.random.uniform(0.5, 2.0, (1, I)) * fi).astype(np.float32),
        "vals": (n((E, T)) / ti[np.arange(E) % 512 // 64]).astype(np.float32),
        "own": ((np.arange(E)[:, None] // 64 == np.arange(Q) % 8) * 1.0).astype(np.float32),
        "offs": striped8(idx),
    }


def reference(query, keys, th, size, vals, own, offs):
    idx = unstriped8(offs)
    kb = pick8(f64(keys), idx, 64).reshape(D, G, I // G).mean(axis=2)
    queryq = mxq(f64(query), 0, "e4m3")
    kbq = mxq(kb, 0, "e4m3")
    b = queryq.T @ kbq
    gate = sigmoid(14.0 * b - f64(th))
    gr = np.repeat(gate, I // G, axis=1)
    keysidxq = mxq(pick8(f64(keys), idx, 64), 0, "e4m3")
    a = queryq.T @ keysidxq
    p = np.exp(a - np.max(a, axis=1, keepdims=True)) * gr
    w = p * f64(size) / np.sum(p, axis=1, keepdims=True)
    wt = w.T
    vt = pick8(f64(vals), idx, 64).T
    vtq = mxq(vt, 0, "e4m3")
    wtq = mxq(wt, 0, "e4m3")
    o = vtq.T @ wtq
    ob = o * f64(own)
    y = ob.reshape(E, X, Q // X).sum(axis=2)
    return y

@@ -1,0 +1,225 @@
+from contextlib import ExitStack
+
+import concourse.mybir as mybir
+from concourse.masks import make_identity
+
+D, T, I, Q, X, E, G = 512, 1024, 512, 256, 32, 512, 64
+FLOPS = 2 * D * Q * G + 2 * D * Q * I + 2 * I * E * Q
+
+F32 = mybir.dt.float32
+BF16 = mybir.dt.bfloat16
+U32 = mybir.dt.uint32
+U16 = mybir.dt.uint16
+U8 = mybir.dt.uint8
+FP8X4 = mybir.dt.float8_e4m3fn_x4
+ACT = mybir.ActivationFunctionType
+ALU = mybir.AluOpType
+AX = mybir.AxisListType
+
+P = 128
+PACK = 4
+BLOCK = I // G
+TILES = Q // P
+SLOPE = 14.0 / BLOCK
+
+
+def tile_attend_ownlists_moba_kernel(tc, query, keys, th, size, vals, own, offs, out):
+    nc = tc.nc
+    with ExitStack() as ctx:
+        keep = ctx.enter_context(tc.tile_pool(name="keep", bufs=1))
+        psum = ctx.enter_context(tc.psum_pool(name="psum", bufs=1))
+
+        def bank(tag, name):
+            return psum.tile([P, 512], F32, tag=tag, name=name)
+
+        def mx_tiles(name, width):
+            codes = keep.tile([P, width], U32, name=name + "_codes", align_bytes=64)
+            scales = keep.tile([P, width], U8, name=name + "_scales", align_bytes=64)
+            return codes, scales
+
+        def quantize(codes, scales, grouped, lo, hi):
+            nc.vector.quantize_mx(out=codes[:, lo:hi].bitcast(FP8X4), scales=scales[:, lo:hi],
+                                  in_=grouped[:, PACK * lo : PACK * hi])
+
+        def product(dst, left, lcols, right, rcols):
+            nc.tensor.matmul_mx(out=dst, lhsT=left[0][:, lcols].bitcast(FP8X4), lhsT_scale=left[1][:, lcols],
+                                rhs=right[0][:, rcols].bitcast(FP8X4), rhs_scale=right[1][:, rcols],
+                                start=True, stop=True)
+
+        lists = keep.tile([P, I // 16], U16, name="lists")
+        key_planes = keys.rearrange("(p t) w -> p t w", t=PACK)
+        val_planes = vals.rearrange("(p t) w -> p t w", t=PACK)
+        key_pool = [keep.tile([P, T], F32, name="key_pool%d" % t) for t in range(PACK)]
+        for t in range(PACK):
+            nc.sync.dma_start(key_pool[t][:], key_planes[:, t, :])
+            if t == 0:
+                nc.sync.dma_start(lists[:], offs)
+        q_raw = keep.tile([P, PACK, Q], F32, name="q_raw")
+        nc.sync.dma_start(q_raw[:], query.rearrange("(p t) q -> p t q", t=PACK))
+        th_col = keep.tile([P, TILES], F32, name="th_col")
+        size_col = keep.tile([P, PACK], F32, name="size_col")
+        with nc.allow_non_contiguous_dma(reason="one threshold for each partition"):
+            nc.sync.dma_start(th_col[:], th.rearrange("(c p) o -> p (c o)", p=P))
+        nc.sync.dma_start(size_col[:], size.rearrange("o (p t) -> p (o t)", t=PACK))
+        val_pool = {}
+        val_raw = {}
+        for pair in range(2):
+            if pair in ():
+                for h in range(2):
+                    val_raw[pair, h] = keep.tile([P, 2, T // 2], F32, name="val_raw%d%d" % (pair, h))
+                    nc.sync.dma_start(val_raw[pair, h][:], val_planes[:, 2 * pair : 2 * pair + 2, h * (T // 2) : (h + 1) * (T // 2)])
+            else:
+                for t in range(2 * pair, 2 * pair + 2):
+                    val_pool[t] = keep.tile([P, T], F32, name="val_pool%d" % t)
+                    nc.sync.dma_start(val_pool[t][:], val_planes[:, t, :])
+        own_sb = keep.tile([P, PACK * Q], F32, name="own_sb")
+        nc.sync.dma_start(own_sb[:], own.rearrange("(p t) q -> p (t q)", t=PACK))
+
+        warm = keep.tile([P, 1], F32, name="warm")
+        nc.vector.memset(warm[:], 0.0)
+        nc.scalar.activation(warm[:], warm[:], ACT.Exp)
+        ident = keep.tile([P, P], F32, name="ident")
+        make_identity(nc, ident[:])
+
+        size_rows = bank("size", "size_rows")
+        for t in range(PACK):
+            nc.tensor.transpose(size_rows[:, t * P : (t + 1) * P], size_col[:, t : t + 1].to_broadcast([P, P]), ident[:])
+
+        k_listed = keep.tile([P, PACK * I], F32, name="k_listed")
+        k_grouped = keep.tile([P, PACK * I], BF16, name="k_grouped", align_bytes=64)
+        kb_grouped = keep.tile([P, PACK * G], BF16, name="kb_grouped", align_bytes=64)
+        kg = k_grouped[:].rearrange("p (i t) -> p i t", t=PACK)
+
+        def k_pair_src(pair, lo, hi):
+            return k_listed[:, 2 * pair * I : (2 * pair + 2) * I].rearrange("p (f i) -> p i f", f=2)[:, lo:hi, :]
+
+        sums_sb = keep.tile([P, 2 * P], F32, name="sums_sb")
+        kb_back = bank("kb_back", "kb_back")
+        for pair in range(2):
+            for t in range(2 * pair, 2 * pair + 2):
+                nc.vector.tensor_copy(k_listed[:, t * I : (t + 1) * I], key_pool[t][:].indirect(lists[:]))
+            if pair == 0:
+                nc.scalar.copy(kg[:, :, 0:2], k_pair_src(0, 0, I))
+            else:
+                if 512 > 0:
+                    nc.vector.tensor_copy(kg[:, 0:512, 2:4], k_pair_src(1, 0, 512))
+                if 512 < I:
+                    nc.scalar.copy(kg[:, 512:I, 2:4], k_pair_src(1, 512, I))
+            if pair in (0, 1):
+                sums = bank("sums%d" % pair, "sums%d" % pair)
+                for r in range(BLOCK):
+                    nc.tensor.matmul(sums[:, 0:P], lhsT=k_listed[:, 2 * pair * I + r : (2 * pair + 2) * I : BLOCK], rhs=ident[:],
+                                     is_transpose=True, start=(r == 0), stop=(r == BLOCK - 1))
+                nc.scalar.copy(sums_sb[:, pair * P : (pair + 1) * P], sums[:, 0:P])
+                nc.tensor.transpose(kb_back[:, pair * P : (pair + 1) * P], sums_sb[:, pair * P : (pair + 1) * P], ident[:])
+            else:
+                with nc.allow_low_precision(reason="float32 sum, one rounding"):
+                    nc.vector.tensor_reduce(kb_grouped[:].rearrange("p (g t) -> p t g", t=PACK)[:, 2 * pair : 2 * pair + 2, :],
+                                            k_listed[:, 2 * pair * I : (2 * pair + 2) * I].rearrange("p (f g r) -> p f g r", f=2, r=BLOCK), AX.X, ALU.add)
+        k_mx = mx_tiles("k", I)
+        quantize(k_mx[0], k_mx[1], k_grouped, 0, I)
+
+        q_grouped = keep.tile([P, PACK * Q], BF16, name="q_grouped", align_bytes=64)
+        q_mx = mx_tiles("q", Q)
+        scores = []
+        for c in range(TILES):
+            nc.scalar.copy(q_grouped[:, c * PACK * P : (c + 1) * PACK * P].rearrange("p (q t) -> p q t", t=PACK),
+                           q_raw[:, :, c * P : (c + 1) * P].rearrange("p t q -> p q t"))
+            quantize(q_mx[0], q_mx[1], q_grouped, c * P, (c + 1) * P)
+            scores.append(bank("scores%d" % c, "scores%d" % c))
+            product(scores[c][:], q_mx, slice(c * P, (c + 1) * P), k_mx, slice(0, I))
+
+        kbg = kb_grouped[:].rearrange("p (g t) -> p g t", t=PACK)
+        if len((0, 1)) == 2:
+            nc.scalar.copy(kbg, kb_back[:, 0 : PACK * G].rearrange("p (t g) -> p g t", t=PACK))
+        else:
+            for pair in range(2):
+                if pair in (0, 1):
+                    nc.scalar.copy(kbg[:, :, 2 * pair : 2 * pair + 2], kb_back[:, pair * P : (pair + 1) * P].rearrange("p (t g) -> p g t", t=2))
+        kb_mx = mx_tiles("kb", G)
+        quantize(kb_mx[0], kb_mx[1], kb_grouped, 0, G)
+        block_scores = bank("block_scores", "block_scores")
+        for c in range(TILES):
+            product(block_scores[:, c * G : (c + 1) * G], q_mx, slice(c * P, (c + 1) * P), kb_mx, slice(0, G))
+
+        v_low = keep.tile([P, TILES * G], F32, name="v_low")
+        v_abs = keep.tile([P, TILES * G], F32, name="v_abs")
+        v_exp = keep.tile([P, TILES * G], F32, name="v_exp")
+        v_tanh = keep.tile([P, TILES * G], F32, name="v_tanh")
+        gate = keep.tile([P, TILES * G], F32, name="gate")
+        for c in range(TILES):
+            cols = slice(c * G, (c + 1) * G)
+            nc.scalar.activation(v_abs[:, cols], block_scores[:, cols], ACT.Abs, bias=th_col[:, c : c + 1], scale=-SLOPE)
+            nc.scalar.activation(v_low[:, cols], block_scores[:, cols], ACT.Relu, bias=th_col[:, c : c + 1], scale=-SLOPE)
+        nc.scalar.activation(v_tanh[:], v_abs[:], ACT.Tanh, scale=0.5)
+        nc.scalar.activation(v_exp[:], v_low[:], ACT.Exp, scale=-1.0)
+        nc.vector.scalar_tensor_tensor(gate[:], v_tanh[:], 1.0, v_exp[:], ALU.add, ALU.mult)
+
+        v_grouped = keep.tile([P, PACK * E], BF16, name="v_grouped", align_bytes=64)
+        v_mx = mx_tiles("v", E)
+
+        def values(pair):
+            turned = bank("v_turned%d" % pair if pair == 0 else "sums0", "v_turned%d" % pair)
+            if pair in ():
+                words = keep.tile([P, T], F32, name="val_words%d" % pair)
+                for h in range(2):
+                    nc.scalar.activation(
+                        words[:, h * (T // 2) : (h + 1) * (T // 2)].bitcast(BF16).rearrange("p (k f e) -> p k f e", f=2, e=2),
+                        val_raw[pair, h][:].rearrange("p f (k e) -> p k f e", e=2), ACT.Copy)
+                listed = keep.tile([P, I], F32, name="v_listed_words%d" % pair)
+                nc.vector.tensor_copy(listed[:], words[:].indirect(lists[:]))
+                for f in range(2):
+                    for u in range(2):
+                        nc.tensor.transpose(turned[:, (2 * f + u) * P : (2 * f + u + 1) * P], listed[:, 2 * u + f : I : 4], ident[:])
+            else:
+                for f in range(2):
+                    listed = keep.tile([P, I], BF16, name="v_listed%d" % (2 * pair + f))
+                    nc.vector.tensor_copy(listed[:], val_pool[2 * pair + f][:].indirect(lists[:]))
+                    for u in range(2):
+                        nc.tensor.transpose(turned[:, (2 * f + u) * P : (2 * f + u + 1) * P], listed[:].bitcast(F32)[:, u : I // 2 : 2], ident[:])
+            nc.scalar.copy(v_grouped[:, pair * 2 * PACK * P : (pair + 1) * 2 * PACK * P].bitcast(F32).rearrange("p (f e u) -> p f e u", f=2, u=2),
+                           turned[:].rearrange("p (f u e) -> p f e u", f=2, u=2))
+            quantize(v_mx[0], v_mx[1], v_grouped, pair * 2 * P, (pair + 1) * 2 * P)
+
+        neg_max = [keep.tile([P, 1], F32, name="neg_max%d" % c) for c in range(TILES)]
+        row_sum = [keep.tile([P, 1], F32, name="row_sum%d" % c) for c in range(TILES)]
+        inv_sum = [keep.tile([P, 1], F32, name="inv_sum%d" % c) for c in range(TILES)]
+        expd = [keep.tile([P, I], F32, name="expd%d" % c) for c in range(TILES)]
+        gated = [keep.tile([P, I], F32, name="gated%d" % c) for c in range(TILES)]
+        w_rows = [keep.tile([P, I], BF16, name="w_rows%d" % c) for c in range(TILES)]
+        w_grouped = keep.tile([P, PACK * Q], BF16, name="w_grouped", align_bytes=64)
+        w_mx = mx_tiles("w", Q)
+        for c in range(TILES):
+            nc.vector.tensor_reduce(neg_max[c][:], scores[c][:], AX.X, ALU.max, negate=True)
+            nc.scalar.activation(expd[c][:], scores[c][:], ACT.Exp, bias=neg_max[c][:], scale=1.0)
+        def weights(c):
+            nc.vector.scalar_tensor_tensor(
+                gated[c][:].rearrange("p (g r) -> p g r", r=BLOCK), expd[c][:].rearrange("p (g r) -> p g r", r=BLOCK), 1.0,
+                gate[:, c * G : (c + 1) * G].unsqueeze(2).to_broadcast([P, G, BLOCK]), ALU.mult, ALU.mult, accum_out=row_sum[c][:])
+            nc.vector.reciprocal(inv_sum[c][:], row_sum[c][:])
+            nc.vector.scalar_tensor_tensor(
+                w_rows[c][:].rearrange("p (s t) -> p s t", t=PACK), gated[c][:].rearrange("p (s t) -> p s t", t=PACK), inv_sum[c][:],
+                size_rows[:].rearrange("p (t s) -> p s t", t=PACK), ALU.mult, ALU.mult)
+            turned = bank("kb_back" if c == 0 else "block_scores", "w_turned%d" % c)
+            for u in range(2):
+                nc.tensor.transpose(turned[:, u * P : (u + 1) * P], w_rows[c][:].bitcast(F32)[:, u : I // 2 : 2], ident[:])
+            nc.scalar.copy(w_grouped[:, c * PACK * P : (c + 1) * PACK * P].bitcast(F32).rearrange("p (q u) -> p q u", u=2),
+                           turned[:, 0 : 2 * P].rearrange("p (u q) -> p q u", u=2))
+            quantize(w_mx[0], w_mx[1], w_grouped, c * P, (c + 1) * P)
+
+        weights(0)
+        weights(1)
+        values(0)
+        values(1)
+
+        result = keep.tile([P, PACK, X], F32, name="result")
+        for c in range(TILES):
+            sums_o = bank("scores%d" % c, "o%d" % c)
+            for t in range(PACK):
+                product(sums_o[:, t * P : (t + 1) * P], v_mx, slice(t * P, (t + 1) * P), w_mx, slice(c * P, (c + 1) * P))
+            kept = keep.tile([P, PACK * P], F32, name="kept%d" % c)
+            nc.vector.tensor_tensor(kept[:].rearrange("p (t q) -> p t q", t=PACK), sums_o[:].rearrange("p (t q) -> p t q", t=PACK),
+                                    own_sb[:].rearrange("p (t q) -> p t q", t=PACK)[:, :, c * P : (c + 1) * P], ALU.mult)
+            nc.vector.tensor_reduce(result[:, :, c * (X // TILES) : (c + 1) * (X // TILES)],
+                                    kept[:].rearrange("p (t x r) -> p t x r", t=PACK, r=Q // X), AX.X, ALU.add)
+        nc.sync.dma_start(out.rearrange("(p t) x -> p t x", t=PACK), result[:])

@@ -20,7 +20,10 @@ P = 128
 PACK = 4
 BLOCK = I // G
 TILES = Q // P
+PAIRS = PACK // 2
 SLOPE = 14.0 / BLOCK
+VECTOR_SLOTS = 192
+WORD_PAIRS = (1,)
 
 
 def tile_attend_ownlists_moba_kernel(tc, query, keys, th, size, vals, own, offs, out):
@@ -32,194 +35,190 @@ def tile_attend_ownlists_moba_kernel(tc, query, keys, th, size, vals, own, offs,
         def bank(tag, name):
             return psum.tile([P, 512], F32, tag=tag, name=name)
 
-        def mx_tiles(name, width):
-            codes = keep.tile([P, width], U32, name=name + "_codes", align_bytes=64)
+        def cols(n, width):
+            return slice(n * width, (n + 1) * width)
+
+        def mx_tiles(name, width, tag=""):
+            codes = keep.tile([P, width], U32, name=name + "_codes", tag=tag, align_bytes=64)
             scales = keep.tile([P, width], U8, name=name + "_scales", align_bytes=64)
             return codes, scales
 
-        def quantize(codes, scales, grouped, lo, hi):
-            nc.vector.quantize_mx(out=codes[:, lo:hi].bitcast(FP8X4), scales=scales[:, lo:hi],
-                                  in_=grouped[:, PACK * lo : PACK * hi])
+        def quantize(operand, grouped, part):
+            nc.vector.quantize_mx(out=operand[0][:, part].bitcast(FP8X4), scales=operand[1][:, part],
+                                  in_=grouped[:, PACK * part.start : PACK * part.stop])
 
-        def product(dst, left, lcols, right, rcols):
-            nc.tensor.matmul_mx(out=dst, lhsT=left[0][:, lcols].bitcast(FP8X4), lhsT_scale=left[1][:, lcols],
-                                rhs=right[0][:, rcols].bitcast(FP8X4), rhs_scale=right[1][:, rcols],
+        def product(dst, left, left_part, right, right_part):
+            nc.tensor.matmul_mx(out=dst, lhsT=left[0][:, left_part].bitcast(FP8X4), lhsT_scale=left[1][:, left_part],
+                                rhs=right[0][:, right_part].bitcast(FP8X4), rhs_scale=right[1][:, right_part],
                                 start=True, stop=True)
 
         lists = keep.tile([P, I // 16], U16, name="lists")
         key_planes = keys.rearrange("(p t) w -> p t w", t=PACK)
         val_planes = vals.rearrange("(p t) w -> p t w", t=PACK)
         key_pool = [keep.tile([P, T], F32, name="key_pool%d" % t) for t in range(PACK)]
-        for t in range(PACK):
-            nc.sync.dma_start(key_pool[t][:], key_planes[:, t, :])
-            if t == 0:
-                nc.sync.dma_start(lists[:], offs)
-        q_raw = keep.tile([P, PACK, Q], F32, name="q_raw")
-        nc.sync.dma_start(q_raw[:], query.rearrange("(p t) q -> p t q", t=PACK))
+        val_pool = {}
+        q_raw = keep.tile([P, PACK, Q], F32, name="q_raw", tag="q_raw")
         th_col = keep.tile([P, TILES], F32, name="th_col")
         size_col = keep.tile([P, PACK], F32, name="size_col")
+        own_sb = keep.tile([P, PACK * Q], F32, name="own_sb")
+
+        def load_values(n):
+            if n // 2 in WORD_PAIRS:
+                val_pool[n] = keep.tile([P, 2, T // 2], F32, name="val_raw%d" % n, tag="val_raw%d" % n)
+                nc.sync.dma_start(val_pool[n][:], val_planes[:, cols(n // 2, 2), cols(n % 2, T // 2)])
+            else:
+                val_pool[n] = keep.tile([P, T], F32, name="val_pool%d" % n)
+                nc.sync.dma_start(val_pool[n][:], val_planes[:, n, :])
+
+        nc.sync.dma_start(key_pool[0][:], key_planes[:, 0, :])
+        nc.sync.dma_start(lists[:], offs)
+        for t in range(1, PACK):
+            nc.sync.dma_start(key_pool[t][:], key_planes[:, t, :])
+        for n in (0,):
+            load_values(n)
+        nc.sync.dma_start(q_raw[:], query.rearrange("(p t) q -> p t q", t=PACK))
+        for n in (2,):
+            load_values(n)
         with nc.allow_non_contiguous_dma(reason="one threshold for each partition"):
             nc.sync.dma_start(th_col[:], th.rearrange("(c p) o -> p (c o)", p=P))
+        for n in (3, 1):
+            load_values(n)
         nc.sync.dma_start(size_col[:], size.rearrange("o (p t) -> p (o t)", t=PACK))
-        val_pool = {}
-        val_raw = {}
-        for pair in range(2):
-            if pair in ():
-                for h in range(2):
-                    val_raw[pair, h] = keep.tile([P, 2, T // 2], F32, name="val_raw%d%d" % (pair, h))
-                    nc.sync.dma_start(val_raw[pair, h][:], val_planes[:, 2 * pair : 2 * pair + 2, h * (T // 2) : (h + 1) * (T // 2)])
-            else:
-                for t in range(2 * pair, 2 * pair + 2):
-                    val_pool[t] = keep.tile([P, T], F32, name="val_pool%d" % t)
-                    nc.sync.dma_start(val_pool[t][:], val_planes[:, t, :])
-        own_sb = keep.tile([P, PACK * Q], F32, name="own_sb")
         nc.sync.dma_start(own_sb[:], own.rearrange("(p t) q -> p (t q)", t=PACK))
 
         warm = keep.tile([P, 1], F32, name="warm")
-        nc.vector.memset(warm[:], 0.0)
+        nc.gpsimd.memset(warm[:], 0.0)
         nc.scalar.activation(warm[:], warm[:], ACT.Exp)
         ident = keep.tile([P, P], F32, name="ident")
         make_identity(nc, ident[:])
 
-        size_rows = bank("size", "size_rows")
-        for t in range(PACK):
-            nc.tensor.transpose(size_rows[:, t * P : (t + 1) * P], size_col[:, t : t + 1].to_broadcast([P, P]), ident[:])
-
         k_listed = keep.tile([P, PACK * I], F32, name="k_listed")
         k_grouped = keep.tile([P, PACK * I], BF16, name="k_grouped", align_bytes=64)
-        kb_grouped = keep.tile([P, PACK * G], BF16, name="kb_grouped", align_bytes=64)
-        kg = k_grouped[:].rearrange("p (i t) -> p i t", t=PACK)
+        sums = bank("sums", "sums")
 
-        def k_pair_src(pair, lo, hi):
-            return k_listed[:, 2 * pair * I : (2 * pair + 2) * I].rearrange("p (f i) -> p i f", f=2)[:, lo:hi, :]
+        def interleave_keys(copy, pair, slots):
+            copy(k_grouped[:].rearrange("p (i t) -> p i t", t=PACK)[:, slots, cols(pair, 2)],
+                 k_listed[:, cols(pair, 2 * I)].rearrange("p (f i) -> p i f", f=2)[:, slots, :])
 
-        sums_sb = keep.tile([P, 2 * P], F32, name="sums_sb")
-        kb_back = bank("kb_back", "kb_back")
-        for pair in range(2):
+        for pair in range(PAIRS):
             for t in range(2 * pair, 2 * pair + 2):
-                nc.vector.tensor_copy(k_listed[:, t * I : (t + 1) * I], key_pool[t][:].indirect(lists[:]))
+                nc.vector.tensor_copy(k_listed[:, cols(t, I)], key_pool[t][:].indirect(lists[:]))
             if pair == 0:
-                nc.scalar.copy(kg[:, :, 0:2], k_pair_src(0, 0, I))
+                interleave_keys(nc.scalar.copy, pair, slice(0, I))
             else:
-                if 512 > 0:
-                    nc.vector.tensor_copy(kg[:, 0:512, 2:4], k_pair_src(1, 0, 512))
-                if 512 < I:
-                    nc.scalar.copy(kg[:, 512:I, 2:4], k_pair_src(1, 512, I))
-            if pair in (0, 1):
-                sums = bank("sums%d" % pair, "sums%d" % pair)
-                for r in range(BLOCK):
-                    nc.tensor.matmul(sums[:, 0:P], lhsT=k_listed[:, 2 * pair * I + r : (2 * pair + 2) * I : BLOCK], rhs=ident[:],
-                                     is_transpose=True, start=(r == 0), stop=(r == BLOCK - 1))
-                nc.scalar.copy(sums_sb[:, pair * P : (pair + 1) * P], sums[:, 0:P])
-                nc.tensor.transpose(kb_back[:, pair * P : (pair + 1) * P], sums_sb[:, pair * P : (pair + 1) * P], ident[:])
-            else:
-                with nc.allow_low_precision(reason="float32 sum, one rounding"):
-                    nc.vector.tensor_reduce(kb_grouped[:].rearrange("p (g t) -> p t g", t=PACK)[:, 2 * pair : 2 * pair + 2, :],
-                                            k_listed[:, 2 * pair * I : (2 * pair + 2) * I].rearrange("p (f g r) -> p f g r", f=2, r=BLOCK), AX.X, ALU.add)
+                interleave_keys(nc.vector.tensor_copy, pair, slice(0, VECTOR_SLOTS))
+                interleave_keys(nc.scalar.copy, pair, slice(VECTOR_SLOTS, I))
+            for r in range(BLOCK):
+                nc.tensor.matmul(sums[:, cols(pair, P)], lhsT=k_listed[:, 2 * pair * I + r : 2 * (pair + 1) * I : BLOCK],
+                                 rhs=ident[:], is_transpose=True, start=(r == 0), stop=(r == BLOCK - 1))
         k_mx = mx_tiles("k", I)
-        quantize(k_mx[0], k_mx[1], k_grouped, 0, I)
+        quantize(k_mx, k_grouped, slice(0, I))
 
+        kb_grouped = keep.tile([P, PACK * G], BF16, name="kb_grouped", align_bytes=64)
+        kb_mx = mx_tiles("kb", G)
         q_grouped = keep.tile([P, PACK * Q], BF16, name="q_grouped", align_bytes=64)
         q_mx = mx_tiles("q", Q)
-        scores = []
+        scores = [bank("scores%d" % c, "scores%d" % c) for c in range(TILES)]
         for c in range(TILES):
-            nc.scalar.copy(q_grouped[:, c * PACK * P : (c + 1) * PACK * P].rearrange("p (q t) -> p q t", t=PACK),
-                           q_raw[:, :, c * P : (c + 1) * P].rearrange("p t q -> p q t"))
-            quantize(q_mx[0], q_mx[1], q_grouped, c * P, (c + 1) * P)
-            scores.append(bank("scores%d" % c, "scores%d" % c))
-            product(scores[c][:], q_mx, slice(c * P, (c + 1) * P), k_mx, slice(0, I))
-
-        kbg = kb_grouped[:].rearrange("p (g t) -> p g t", t=PACK)
-        if len((0, 1)) == 2:
-            nc.scalar.copy(kbg, kb_back[:, 0 : PACK * G].rearrange("p (t g) -> p g t", t=PACK))
-        else:
-            for pair in range(2):
-                if pair in (0, 1):
-                    nc.scalar.copy(kbg[:, :, 2 * pair : 2 * pair + 2], kb_back[:, pair * P : (pair + 1) * P].rearrange("p (t g) -> p g t", t=2))
-        kb_mx = mx_tiles("kb", G)
-        quantize(kb_mx[0], kb_mx[1], kb_grouped, 0, G)
+            nc.scalar.copy(q_grouped[:, cols(c, PACK * P)].rearrange("p (q t) -> p q t", t=PACK),
+                           q_raw[:, :, cols(c, P)].rearrange("p t q -> p q t"))
+            quantize(q_mx, q_grouped, cols(c, P))
+        sums_sb = keep.tile([P, PAIRS * P], F32, name="sums_sb", tag="q_raw")
+        nc.scalar.copy(sums_sb[:], sums[:, 0 : PAIRS * P])
+        sums_back = bank("sums_back", "sums_back")
+        for pair in range(PAIRS):
+            nc.tensor.transpose(sums_back[:, cols(pair, P)], sums_sb[:, cols(pair, P)], ident[:])
+        nc.scalar.copy(kb_grouped[:].rearrange("p (g t) -> p g t", t=PACK),
+                       sums_back[:, 0 : PACK * G].rearrange("p (t g) -> p g t", t=PACK))
+        quantize(kb_mx, kb_grouped, slice(0, G))
         block_scores = bank("block_scores", "block_scores")
         for c in range(TILES):
-            product(block_scores[:, c * G : (c + 1) * G], q_mx, slice(c * P, (c + 1) * P), kb_mx, slice(0, G))
-
-        v_low = keep.tile([P, TILES * G], F32, name="v_low")
-        v_abs = keep.tile([P, TILES * G], F32, name="v_abs")
-        v_exp = keep.tile([P, TILES * G], F32, name="v_exp")
-        v_tanh = keep.tile([P, TILES * G], F32, name="v_tanh")
-        gate = keep.tile([P, TILES * G], F32, name="gate")
+            product(block_scores[:, cols(c, G)], q_mx, cols(c, P), kb_mx, slice(0, G))
         for c in range(TILES):
-            cols = slice(c * G, (c + 1) * G)
-            nc.scalar.activation(v_abs[:, cols], block_scores[:, cols], ACT.Abs, bias=th_col[:, c : c + 1], scale=-SLOPE)
-            nc.scalar.activation(v_low[:, cols], block_scores[:, cols], ACT.Relu, bias=th_col[:, c : c + 1], scale=-SLOPE)
-        nc.scalar.activation(v_tanh[:], v_abs[:], ACT.Tanh, scale=0.5)
-        nc.scalar.activation(v_exp[:], v_low[:], ACT.Exp, scale=-1.0)
-        nc.vector.scalar_tensor_tensor(gate[:], v_tanh[:], 1.0, v_exp[:], ALU.add, ALU.mult)
+            product(scores[c][:], q_mx, cols(c, P), k_mx, slice(0, I))
 
-        v_grouped = keep.tile([P, PACK * E], BF16, name="v_grouped", align_bytes=64)
-        v_mx = mx_tiles("v", E)
+        v_low = [keep.tile([P, G], F32, name="v_low%d" % c, tag="low%d" % c, align_bytes=64) for c in range(TILES)]
+        v_abs = [keep.tile([P, G], F32, name="v_abs%d" % c) for c in range(TILES)]
+        v_exp = [keep.tile([P, G], F32, name="v_exp%d" % c) for c in range(TILES)]
+        v_tanh = [keep.tile([P, G], F32, name="v_tanh%d" % c) for c in range(TILES)]
+        gate = [keep.tile([P, G], F32, name="gate%d" % c) for c in range(TILES)]
+        neg_max = [keep.tile([P, 1], F32, name="neg_max%d" % c) for c in range(TILES)]
+        row_sum = [keep.tile([P, 1], F32, name="row_sum%d" % c) for c in range(TILES)]
+        inv_sum = [keep.tile([P, 1], F32, name="inv_sum%d" % c) for c in range(TILES)]
+        gated = [keep.tile([P, I], F32, name="gated%d" % c, tag="gated%d" % c, align_bytes=64) for c in range(TILES)]
+        w_rows = [keep.tile([P, I], BF16, name="w_rows%d" % c) for c in range(TILES)]
+        for c in range(TILES):
+            nc.scalar.activation(v_abs[c][:], block_scores[:, cols(c, G)], ACT.Abs, bias=th_col[:, c : c + 1], scale=-SLOPE)
+            nc.scalar.activation(v_low[c][:], block_scores[:, cols(c, G)], ACT.Relu, bias=th_col[:, c : c + 1], scale=-SLOPE)
+        for c in range(TILES):
+            nc.scalar.activation(v_tanh[c][:], v_abs[c][:], ACT.Tanh, scale=0.5)
+            nc.scalar.activation(v_exp[c][:], v_low[c][:], ACT.Exp, scale=-1.0)
+            nc.vector.scalar_tensor_tensor(gate[c][:], v_tanh[c][:], 1.0, v_exp[c][:], ALU.add, ALU.mult)
+        words = {}
+        for pair in WORD_PAIRS:
+            words[pair] = keep.tile([P, T], F32, name="val_words%d" % pair)
+            for n in range(4):
+                h, part = divmod(n, 4 // 2)
+                width = T // 4
+                nc.scalar.activation(words[pair][:, cols(n, width)].bitcast(BF16).rearrange("p (k f e) -> p k f e", f=2, e=2),
+                                     val_pool[2 * pair + h][:, :, cols(part, width)].rearrange("p f (k e) -> p k f e", e=2), ACT.Copy)
+        expd = keep.tile([P, TILES * I], F32, name="expd", tag="val_raw3")
+        for c in range(TILES):
+            nc.vector.tensor_reduce(neg_max[c][:], scores[c][:], AX.X, ALU.max, negate=True)
+            nc.scalar.activation(expd[:, cols(c, I)], scores[c][:], ACT.Exp, bias=neg_max[c][:], scale=1.0)
 
-        def values(pair):
-            turned = bank("v_turned%d" % pair if pair == 0 else "sums0", "v_turned%d" % pair)
-            if pair in ():
-                words = keep.tile([P, T], F32, name="val_words%d" % pair)
-                for h in range(2):
-                    nc.scalar.activation(
-                        words[:, h * (T // 2) : (h + 1) * (T // 2)].bitcast(BF16).rearrange("p (k f e) -> p k f e", f=2, e=2),
-                        val_raw[pair, h][:].rearrange("p f (k e) -> p k f e", e=2), ACT.Copy)
+        size_rows = bank("block_scores", "size_rows")
+        for t in range(PACK):
+            nc.tensor.transpose(size_rows[:, cols(t, P)], size_col[:, t : t + 1].to_broadcast([P, P]), ident[:])
+        w_grouped = keep.tile([P, PACK * Q], BF16, name="w_grouped", align_bytes=64)
+        w_mx = mx_tiles("w", Q)
+        for c in range(TILES):
+            nc.vector.scalar_tensor_tensor(
+                gated[c][:].rearrange("p (g r) -> p g r", r=BLOCK), expd[:, cols(c, I)].rearrange("p (g r) -> p g r", r=BLOCK), 1.0,
+                gate[c][:].unsqueeze(2).to_broadcast([P, G, BLOCK]), ALU.mult, ALU.mult, accum_out=row_sum[c][:])
+        for c in range(TILES):
+            nc.vector.reciprocal(inv_sum[c][:], row_sum[c][:])
+        for c in range(TILES):
+            nc.vector.scalar_tensor_tensor(
+                w_rows[c][:].rearrange("p (s t) -> p s t", t=PACK), gated[c][:].rearrange("p (s t) -> p s t", t=PACK),
+                inv_sum[c][:], size_rows[:].rearrange("p (t s) -> p s t", t=PACK), ALU.mult, ALU.mult)
+        for c in range(TILES):
+            turned = bank(("sums", "sums_back")[c], "w_turned%d" % c)
+            for u in range(2):
+                nc.tensor.transpose(turned[:, cols(u, P)], w_rows[c][:].bitcast(F32)[:, u : I // 2 : 2], ident[:])
+            nc.scalar.copy(w_grouped[:, cols(c, PACK * P)].bitcast(F32).rearrange("p (q u) -> p q u", u=2),
+                           turned[:, 0 : 2 * P].rearrange("p (u q) -> p q u", u=2))
+            quantize(w_mx, w_grouped, cols(c, P))
+
+        v_grouped = keep.tile([P, PACK * E], BF16, name="v_grouped", tag="low1", align_bytes=64)
+        for pair in (1, 0):
+            turned = bank("v_turned%d" % pair, "v_turned%d" % pair)
+            if pair in WORD_PAIRS:
                 listed = keep.tile([P, I], F32, name="v_listed_words%d" % pair)
-                nc.vector.tensor_copy(listed[:], words[:].indirect(lists[:]))
+                nc.vector.tensor_copy(listed[:], words[pair][:].indirect(lists[:]))
                 for f in range(2):
                     for u in range(2):
-                        nc.tensor.transpose(turned[:, (2 * f + u) * P : (2 * f + u + 1) * P], listed[:, 2 * u + f : I : 4], ident[:])
+                        nc.tensor.transpose(turned[:, cols(2 * f + u, P)], listed[:, 2 * u + f : I : 4], ident[:])
             else:
                 for f in range(2):
                     listed = keep.tile([P, I], BF16, name="v_listed%d" % (2 * pair + f))
                     nc.vector.tensor_copy(listed[:], val_pool[2 * pair + f][:].indirect(lists[:]))
                     for u in range(2):
-                        nc.tensor.transpose(turned[:, (2 * f + u) * P : (2 * f + u + 1) * P], listed[:].bitcast(F32)[:, u : I // 2 : 2], ident[:])
-            nc.scalar.copy(v_grouped[:, pair * 2 * PACK * P : (pair + 1) * 2 * PACK * P].bitcast(F32).rearrange("p (f e u) -> p f e u", f=2, u=2),
+                        nc.tensor.transpose(turned[:, cols(2 * f + u, P)], listed[:].bitcast(F32)[:, u : I // 2 : 2], ident[:])
+            nc.scalar.copy(v_grouped[:, cols(pair, 2 * PACK * P)].bitcast(F32).rearrange("p (f e u) -> p f e u", f=2, u=2),
                            turned[:].rearrange("p (f u e) -> p f e u", f=2, u=2))
-            quantize(v_mx[0], v_mx[1], v_grouped, pair * 2 * P, (pair + 1) * 2 * P)
-
-        neg_max = [keep.tile([P, 1], F32, name="neg_max%d" % c) for c in range(TILES)]
-        row_sum = [keep.tile([P, 1], F32, name="row_sum%d" % c) for c in range(TILES)]
-        inv_sum = [keep.tile([P, 1], F32, name="inv_sum%d" % c) for c in range(TILES)]
-        expd = [keep.tile([P, I], F32, name="expd%d" % c) for c in range(TILES)]
-        gated = [keep.tile([P, I], F32, name="gated%d" % c) for c in range(TILES)]
-        w_rows = [keep.tile([P, I], BF16, name="w_rows%d" % c) for c in range(TILES)]
-        w_grouped = keep.tile([P, PACK * Q], BF16, name="w_grouped", align_bytes=64)
-        w_mx = mx_tiles("w", Q)
-        for c in range(TILES):
-            nc.vector.tensor_reduce(neg_max[c][:], scores[c][:], AX.X, ALU.max, negate=True)
-            nc.scalar.activation(expd[c][:], scores[c][:], ACT.Exp, bias=neg_max[c][:], scale=1.0)
-        def weights(c):
-            nc.vector.scalar_tensor_tensor(
-                gated[c][:].rearrange("p (g r) -> p g r", r=BLOCK), expd[c][:].rearrange("p (g r) -> p g r", r=BLOCK), 1.0,
-                gate[:, c * G : (c + 1) * G].unsqueeze(2).to_broadcast([P, G, BLOCK]), ALU.mult, ALU.mult, accum_out=row_sum[c][:])
-            nc.vector.reciprocal(inv_sum[c][:], row_sum[c][:])
-            nc.vector.scalar_tensor_tensor(
-                w_rows[c][:].rearrange("p (s t) -> p s t", t=PACK), gated[c][:].rearrange("p (s t) -> p s t", t=PACK), inv_sum[c][:],
-                size_rows[:].rearrange("p (t s) -> p s t", t=PACK), ALU.mult, ALU.mult)
-            turned = bank("kb_back" if c == 0 else "block_scores", "w_turned%d" % c)
-            for u in range(2):
-                nc.tensor.transpose(turned[:, u * P : (u + 1) * P], w_rows[c][:].bitcast(F32)[:, u : I // 2 : 2], ident[:])
-            nc.scalar.copy(w_grouped[:, c * PACK * P : (c + 1) * PACK * P].bitcast(F32).rearrange("p (q u) -> p q u", u=2),
-                           turned[:, 0 : 2 * P].rearrange("p (u q) -> p q u", u=2))
-            quantize(w_mx[0], w_mx[1], w_grouped, c * P, (c + 1) * P)
-
-        weights(0)
-        weights(1)
-        values(0)
-        values(1)
+        v_mx = mx_tiles("v", E, tag="gated0")
+        quantize(v_mx, v_grouped, slice(0, E))
 
         result = keep.tile([P, PACK, X], F32, name="result")
+        kept = [keep.tile([P, PACK * P], F32, name="kept%d" % c) for c in range(TILES)]
         for c in range(TILES):
-            sums_o = bank("scores%d" % c, "o%d" % c)
+            mixed = bank("scores%d" % c, "mixed%d" % c)
             for t in range(PACK):
-                product(sums_o[:, t * P : (t + 1) * P], v_mx, slice(t * P, (t + 1) * P), w_mx, slice(c * P, (c + 1) * P))
-            kept = keep.tile([P, PACK * P], F32, name="kept%d" % c)
-            nc.vector.tensor_tensor(kept[:].rearrange("p (t q) -> p t q", t=PACK), sums_o[:].rearrange("p (t q) -> p t q", t=PACK),
-                                    own_sb[:].rearrange("p (t q) -> p t q", t=PACK)[:, :, c * P : (c + 1) * P], ALU.mult)
-            nc.vector.tensor_reduce(result[:, :, c * (X // TILES) : (c + 1) * (X // TILES)],
-                                    kept[:].rearrange("p (t x r) -> p t x r", t=PACK, r=Q // X), AX.X, ALU.add)
+                product(mixed[:, cols(t, P)], v_mx, cols(t, P), w_mx, cols(c, P))
+            nc.vector.tensor_tensor(kept[c][:].rearrange("p (t q) -> p t q", t=PACK), mixed[:].rearrange("p (t q) -> p t q", t=PACK),
+                                    own_sb[:].rearrange("p (t q) -> p t q", t=PACK)[:, :, cols(c, P)], ALU.mult)
+        for c in range(TILES):
+            nc.vector.tensor_reduce(result[:, :, cols(c, X // TILES)],
+                                    kept[c][:].rearrange("p (t x r) -> p t x r", t=PACK, r=Q // X), AX.X, ALU.add)
         nc.sync.dma_start(out.rearrange("(p t) x -> p t x", t=PACK), result[:])

@@ -22,7 +22,7 @@ BLOCK = I // G
 TILES = Q // P
 PAIRS = PACK // 2
 SLOPE = 14.0 / BLOCK
-VECTOR_SLOTS = 192
+VECTOR_SLOTS = 320
 WORD_PAIRS = (1,)
 
 
@@ -74,16 +74,16 @@ def tile_attend_ownlists_moba_kernel(tc, query, keys, th, size, vals, own, offs,
         nc.sync.dma_start(lists[:], offs)
         for t in range(1, PACK):
             nc.sync.dma_start(key_pool[t][:], key_planes[:, t, :])
-        for n in (0,):
+        for n in ():
             load_values(n)
         nc.sync.dma_start(q_raw[:], query.rearrange("(p t) q -> p t q", t=PACK))
-        for n in (2,):
+        for n in ():
             load_values(n)
         with nc.allow_non_contiguous_dma(reason="one threshold for each partition"):
             nc.sync.dma_start(th_col[:], th.rearrange("(c p) o -> p (c o)", p=P))
-        for n in (3, 1):
-            load_values(n)
         nc.sync.dma_start(size_col[:], size.rearrange("o (p t) -> p (o t)", t=PACK))
+        for n in (2, 0, 3, 1):
+            load_values(n)
         nc.sync.dma_start(own_sb[:], own.rearrange("(p t) q -> p (t q)", t=PACK))
 
         warm = keep.tile([P, 1], F32, name="warm")
@@ -108,13 +108,17 @@ def tile_attend_ownlists_moba_kernel(tc, query, keys, th, size, vals, own, offs,
             else:
                 interleave_keys(nc.vector.tensor_copy, pair, slice(0, VECTOR_SLOTS))
                 interleave_keys(nc.scalar.copy, pair, slice(VECTOR_SLOTS, I))
-            for r in range(BLOCK):
-                nc.tensor.matmul(sums[:, cols(pair, P)], lhsT=k_listed[:, 2 * pair * I + r : 2 * (pair + 1) * I : BLOCK],
-                                 rhs=ident[:], is_transpose=True, start=(r == 0), stop=(r == BLOCK - 1))
+            if pair == 0:
+                for r in range(BLOCK):
+                    nc.tensor.matmul(sums[:, 0:P], lhsT=k_listed[:, r : 2 * I : BLOCK],
+                                     rhs=ident[:], is_transpose=True, start=(r == 0), stop=(r == BLOCK - 1))
+        kb_grouped = keep.tile([P, PACK * G], BF16, name="kb_grouped", align_bytes=64)
+        with nc.allow_low_precision(reason="float32 sums, rounded once"):
+            nc.vector.tensor_reduce(kb_grouped[:].rearrange("p (g t) -> p g t", t=PACK)[:, :, 2:4],
+                                    k_listed[:, 2 * I : 4 * I].rearrange("p (f g r) -> p g f r", f=2, r=BLOCK), AX.X, ALU.add)
         k_mx = mx_tiles("k", I)
         quantize(k_mx, k_grouped, slice(0, I))
 
-        kb_grouped = keep.tile([P, PACK * G], BF16, name="kb_grouped", align_bytes=64)
         kb_mx = mx_tiles("kb", G)
         q_grouped = keep.tile([P, PACK * Q], BF16, name="q_grouped", align_bytes=64)
         q_mx = mx_tiles("q", Q)
@@ -123,13 +127,12 @@ def tile_attend_ownlists_moba_kernel(tc, query, keys, th, size, vals, own, offs,
             nc.scalar.copy(q_grouped[:, cols(c, PACK * P)].rearrange("p (q t) -> p q t", t=PACK),
                            q_raw[:, :, cols(c, P)].rearrange("p t q -> p q t"))
             quantize(q_mx, q_grouped, cols(c, P))
-        sums_sb = keep.tile([P, PAIRS * P], F32, name="sums_sb", tag="q_raw")
-        nc.scalar.copy(sums_sb[:], sums[:, 0 : PAIRS * P])
+        sums_sb = keep.tile([P, P], F32, name="sums_sb", tag="q_raw")
+        nc.scalar.copy(sums_sb[:], sums[:, 0:P])
         sums_back = bank("sums_back", "sums_back")
-        for pair in range(PAIRS):
-            nc.tensor.transpose(sums_back[:, cols(pair, P)], sums_sb[:, cols(pair, P)], ident[:])
-        nc.scalar.copy(kb_grouped[:].rearrange("p (g t) -> p g t", t=PACK),
-                       sums_back[:, 0 : PACK * G].rearrange("p (t g) -> p g t", t=PACK))
+        nc.tensor.transpose(sums_back[:, 0:P], sums_sb[:], ident[:])
+        nc.scalar.copy(kb_grouped[:].rearrange("p (g t) -> p g t", t=PACK)[:, :, 0:2],
+                       sums_back[:, 0:P].rearrange("p (f g) -> p g f", f=2))
         quantize(kb_mx, kb_grouped, slice(0, G))
         block_scores = bank("block_scores", "block_scores")
         for c in range(TILES):
@@ -167,7 +170,7 @@ def tile_attend_ownlists_moba_kernel(tc, query, keys, th, size, vals, own, offs,
             nc.vector.tensor_reduce(neg_max[c][:], scores[c][:], AX.X, ALU.max, negate=True)
             nc.scalar.activation(expd[:, cols(c, I)], scores[c][:], ACT.Exp, bias=neg_max[c][:], scale=1.0)
 
-        size_rows = bank("block_scores", "size_rows")
+        size_rows = bank("size_rows", "size_rows")
         for t in range(PACK):
             nc.tensor.transpose(size_rows[:, cols(t, P)], size_col[:, t : t + 1].to_broadcast([P, P]), ident[:])
         w_grouped = keep.tile([P, PACK * Q], BF16, name="w_grouped", align_bytes=64)
@@ -179,13 +182,15 @@ def tile_attend_ownlists_moba_kernel(tc, query, keys, th, size, vals, own, offs,
         for c in range(TILES):
             nc.vector.reciprocal(inv_sum[c][:], row_sum[c][:])
         for c in range(TILES):
-            nc.vector.scalar_tensor_tensor(
-                w_rows[c][:].rearrange("p (s t) -> p s t", t=PACK), gated[c][:].rearrange("p (s t) -> p s t", t=PACK),
-                inv_sum[c][:], size_rows[:].rearrange("p (t s) -> p s t", t=PACK), ALU.mult, ALU.mult)
+            for u in range(2):
+                nc.vector.scalar_tensor_tensor(
+                    w_rows[c][:, cols(u, 2 * P)].rearrange("p (s e) -> p s e", e=2),
+                    gated[c][:].rearrange("p (s t) -> p s t", t=PACK)[:, :, cols(u, 2)], inv_sum[c][:],
+                    size_rows[:, cols(u, 2 * P)].rearrange("p (e s) -> p s e", e=2), ALU.mult, ALU.mult)
         for c in range(TILES):
             turned = bank(("sums", "sums_back")[c], "w_turned%d" % c)
             for u in range(2):
-                nc.tensor.transpose(turned[:, cols(u, P)], w_rows[c][:].bitcast(F32)[:, u : I // 2 : 2], ident[:])
+                nc.tensor.transpose(turned[:, cols(u, P)], w_rows[c][:].bitcast(F32)[:, cols(u, P)], ident[:])
             nc.scalar.copy(w_grouped[:, cols(c, PACK * P)].bitcast(F32).rearrange("p (q u) -> p q u", u=2),
                            turned[:, 0 : 2 * P].rearrange("p (u q) -> p q u", u=2))
             quantize(w_mx, w_grouped, cols(c, P))

@@ -20,10 +20,15 @@ P = 128
 PACK = 4
 BLOCK = I // G
 TILES = Q // P
-PAIRS = PACK // 2
+BANK = 512
 SLOPE = 14.0 / BLOCK
-VECTOR_SLOTS = 320
-WORD_PAIRS = (1,)
+VECTOR_SLOTS = I // 2
+RUN = 4
+CAST_PIECES = 2
+
+
+def cols(n, width):
+    return slice(n * width, (n + 1) * width)
 
 
 def tile_attend_ownlists_moba_kernel(tc, query, keys, th, size, vals, own, offs, out):
@@ -33,10 +38,7 @@ def tile_attend_ownlists_moba_kernel(tc, query, keys, th, size, vals, own, offs,
         psum = ctx.enter_context(tc.psum_pool(name="psum", bufs=1))
 
         def bank(tag, name):
-            return psum.tile([P, 512], F32, tag=tag, name=name)
-
-        def cols(n, width):
-            return slice(n * width, (n + 1) * width)
+            return psum.tile([P, BANK], F32, tag=tag, name=name)
 
         def mx_tiles(name, width, tag=""):
             codes = keep.tile([P, width], U32, name=name + "_codes", tag=tag, align_bytes=64)
@@ -56,129 +58,122 @@ def tile_attend_ownlists_moba_kernel(tc, query, keys, th, size, vals, own, offs,
         key_planes = keys.rearrange("(p t) w -> p t w", t=PACK)
         val_planes = vals.rearrange("(p t) w -> p t w", t=PACK)
         key_pool = [keep.tile([P, T], F32, name="key_pool%d" % t) for t in range(PACK)]
-        val_pool = {}
-        q_raw = keep.tile([P, PACK, Q], F32, name="q_raw", tag="q_raw")
+        val_pool = [keep.tile([P, T], F32, name="val_pool%d" % t) for t in range(2)]
+        val_half = [keep.tile([P, 2, T // 2], F32, name="val_half%d" % h, tag="val_half%d" % h) for h in range(2)]
+        q_raw = keep.tile([P, PACK, Q], F32, name="q_raw")
         th_col = keep.tile([P, TILES], F32, name="th_col")
         size_col = keep.tile([P, PACK], F32, name="size_col")
-        own_sb = keep.tile([P, PACK * Q], F32, name="own_sb")
-
-        def load_values(n):
-            if n // 2 in WORD_PAIRS:
-                val_pool[n] = keep.tile([P, 2, T // 2], F32, name="val_raw%d" % n, tag="val_raw%d" % n)
-                nc.sync.dma_start(val_pool[n][:], val_planes[:, cols(n // 2, 2), cols(n % 2, T // 2)])
-            else:
-                val_pool[n] = keep.tile([P, T], F32, name="val_pool%d" % n)
-                nc.sync.dma_start(val_pool[n][:], val_planes[:, n, :])
+        own_sb = keep.tile([P, PACK, Q], F32, name="own_sb")
 
         nc.sync.dma_start(key_pool[0][:], key_planes[:, 0, :])
         nc.sync.dma_start(lists[:], offs)
         for t in range(1, PACK):
             nc.sync.dma_start(key_pool[t][:], key_planes[:, t, :])
-        for n in ():
-            load_values(n)
         nc.sync.dma_start(q_raw[:], query.rearrange("(p t) q -> p t q", t=PACK))
-        for n in ():
-            load_values(n)
-        with nc.allow_non_contiguous_dma(reason="one threshold for each partition"):
+        nc.sync.dma_start(val_pool[0][:], val_planes[:, 0, :])
+        with nc.allow_non_contiguous_dma(reason="one threshold for each partition of a query tile"):
             nc.sync.dma_start(th_col[:], th.rearrange("(c p) o -> p (c o)", p=P))
-        nc.sync.dma_start(size_col[:], size.rearrange("o (p t) -> p (o t)", t=PACK))
-        for n in (2, 0, 3, 1):
-            load_values(n)
-        nc.sync.dma_start(own_sb[:], own.rearrange("(p t) q -> p (t q)", t=PACK))
+        nc.sync.dma_start(size_col[:], size.rearrange("o (s t) -> s (o t)", t=PACK))
+        for h in range(2):
+            nc.sync.dma_start(val_half[h][:], val_planes[:, 2:4, cols(h, T // 2)])
+        nc.sync.dma_start(val_pool[1][:], val_planes[:, 1, :])
+        nc.sync.dma_start(own_sb[:], own.rearrange("(p t) q -> p t q", t=PACK))
 
-        warm = keep.tile([P, 1], F32, name="warm")
-        nc.gpsimd.memset(warm[:], 0.0)
-        nc.scalar.activation(warm[:], warm[:], ACT.Exp)
         ident = keep.tile([P, P], F32, name="ident")
         make_identity(nc, ident[:])
 
-        k_listed = keep.tile([P, PACK * I], F32, name="k_listed")
+        k_listed = keep.tile([P, PACK * I], F32, name="k_listed", tag="k_listed")
         k_grouped = keep.tile([P, PACK * I], BF16, name="k_grouped", align_bytes=64)
-        sums = bank("sums", "sums")
+
+        def gather_keys(pair):
+            for t in range(2 * pair, 2 * pair + 2):
+                nc.vector.tensor_copy(k_listed[:, cols(t, I)], key_pool[t][:].indirect(lists[:]))
 
         def interleave_keys(copy, pair, slots):
             copy(k_grouped[:].rearrange("p (i t) -> p i t", t=PACK)[:, slots, cols(pair, 2)],
                  k_listed[:, cols(pair, 2 * I)].rearrange("p (f i) -> p i f", f=2)[:, slots, :])
 
-        for pair in range(PAIRS):
-            for t in range(2 * pair, 2 * pair + 2):
-                nc.vector.tensor_copy(k_listed[:, cols(t, I)], key_pool[t][:].indirect(lists[:]))
-            if pair == 0:
-                interleave_keys(nc.scalar.copy, pair, slice(0, I))
-            else:
-                interleave_keys(nc.vector.tensor_copy, pair, slice(0, VECTOR_SLOTS))
-                interleave_keys(nc.scalar.copy, pair, slice(VECTOR_SLOTS, I))
-            if pair == 0:
-                for r in range(BLOCK):
-                    nc.tensor.matmul(sums[:, 0:P], lhsT=k_listed[:, r : 2 * I : BLOCK],
-                                     rhs=ident[:], is_transpose=True, start=(r == 0), stop=(r == BLOCK - 1))
-        kb_grouped = keep.tile([P, PACK * G], BF16, name="kb_grouped", align_bytes=64)
-        with nc.allow_low_precision(reason="float32 sums, rounded once"):
-            nc.vector.tensor_reduce(kb_grouped[:].rearrange("p (g t) -> p g t", t=PACK)[:, :, 2:4],
-                                    k_listed[:, 2 * I : 4 * I].rearrange("p (f g r) -> p g f r", f=2, r=BLOCK), AX.X, ALU.add)
+        gather_keys(0)
+        interleave_keys(nc.scalar.copy, 0, slice(0, I))
+        sums = bank("sums", "sums")
+        for r in range(BLOCK):
+            nc.tensor.matmul(sums[:, 0:P], lhsT=k_listed[:, r : 2 * I : BLOCK], rhs=ident[:],
+                             is_transpose=True, start=(r == 0), stop=(r == BLOCK - 1))
+        gather_keys(1)
+        interleave_keys(nc.vector.tensor_copy, 1, slice(0, VECTOR_SLOTS))
+        interleave_keys(nc.scalar.copy, 1, slice(VECTOR_SLOTS, I))
+        kb_grouped = keep.tile([P, PACK * G], BF16, name="kb_grouped", tag="kb_grouped", align_bytes=64)
+        kb_places = kb_grouped[:].rearrange("p (g t) -> p g t", t=PACK)
+        with nc.allow_low_precision(reason="float32 sums, rounded once on the way to the quantiser"):
+            nc.vector.tensor_reduce(kb_places[:, :, 2:4],
+                                    k_listed[:, 2 * I : 4 * I].rearrange("p (f g r) -> p g f r", f=2, r=BLOCK),
+                                    AX.X, ALU.add)
         k_mx = mx_tiles("k", I)
         quantize(k_mx, k_grouped, slice(0, I))
 
-        kb_mx = mx_tiles("kb", G)
         q_grouped = keep.tile([P, PACK * Q], BF16, name="q_grouped", align_bytes=64)
         q_mx = mx_tiles("q", Q)
-        scores = [bank("scores%d" % c, "scores%d" % c) for c in range(TILES)]
         for c in range(TILES):
-            nc.scalar.copy(q_grouped[:, cols(c, PACK * P)].rearrange("p (q t) -> p q t", t=PACK),
-                           q_raw[:, :, cols(c, P)].rearrange("p t q -> p q t"))
+            nc.scalar.copy(q_grouped[:, cols(c, PACK * P)].rearrange("p (n i t) -> p n t i", i=RUN, t=PACK),
+                           q_raw[:, :, cols(c, P)].rearrange("p t (n i) -> p n t i", i=RUN))
             quantize(q_mx, q_grouped, cols(c, P))
-        sums_sb = keep.tile([P, P], F32, name="sums_sb", tag="q_raw")
+        sums_sb = keep.tile([P, P], F32, name="sums_sb", tag="k_listed")
         nc.scalar.copy(sums_sb[:], sums[:, 0:P])
         sums_back = bank("sums_back", "sums_back")
         nc.tensor.transpose(sums_back[:, 0:P], sums_sb[:], ident[:])
-        nc.scalar.copy(kb_grouped[:].rearrange("p (g t) -> p g t", t=PACK)[:, :, 0:2],
-                       sums_back[:, 0:P].rearrange("p (f g) -> p g f", f=2))
+        nc.scalar.copy(kb_places[:, :, 0:2], sums_back[:, 0:P].rearrange("p (f g) -> p g f", f=2))
+        kb_mx = mx_tiles("kb", G)
         quantize(kb_mx, kb_grouped, slice(0, G))
         block_scores = bank("block_scores", "block_scores")
         for c in range(TILES):
             product(block_scores[:, cols(c, G)], q_mx, cols(c, P), kb_mx, slice(0, G))
+        scores = [bank("scores%d" % c, "scores%d" % c) for c in range(TILES)]
         for c in range(TILES):
             product(scores[c][:], q_mx, cols(c, P), k_mx, slice(0, I))
 
-        v_low = [keep.tile([P, G], F32, name="v_low%d" % c, tag="low%d" % c, align_bytes=64) for c in range(TILES)]
-        v_abs = [keep.tile([P, G], F32, name="v_abs%d" % c) for c in range(TILES)]
-        v_exp = [keep.tile([P, G], F32, name="v_exp%d" % c) for c in range(TILES)]
-        v_tanh = [keep.tile([P, G], F32, name="v_tanh%d" % c) for c in range(TILES)]
-        gate = [keep.tile([P, G], F32, name="gate%d" % c) for c in range(TILES)]
+        val_words = keep.tile([P, T], F32, name="val_words")
+        width = T // (2 * CAST_PIECES)
+        for h in range(2):
+            for piece in range(CAST_PIECES):
+                nc.scalar.activation(
+                    val_words[:, cols(h * CAST_PIECES + piece, width)].bitcast(BF16).rearrange("p (k f e) -> p k f e", f=2, e=2),
+                    val_half[h][:, :, cols(piece, width)].rearrange("p f (k e) -> p k f e", e=2), ACT.Copy)
+
+        gate_in = keep.tile([P, 2, TILES * G], F32, name="gate_in", tag="val_half1")
+        gate_exp = keep.tile([P, TILES * G], F32, name="gate_exp", tag="gate_exp", align_bytes=64)
+        gate_tanh = keep.tile([P, TILES * G], F32, name="gate_tanh")
+        gate = keep.tile([P, TILES * G], F32, name="gate")
+        for c in range(TILES):
+            for n, func in enumerate((ACT.Abs, ACT.Relu)):
+                nc.scalar.activation(gate_in[:, n, cols(c, G)], block_scores[:, cols(c, G)], func,
+                                     bias=th_col[:, c : c + 1], scale=-SLOPE)
+        nc.scalar.activation(gate_tanh[:], gate_in[:, 0, :], ACT.Tanh, scale=0.5)
+        nc.scalar.activation(gate_exp[:], gate_in[:, 1, :], ACT.Exp, scale=-1.0)
+        nc.vector.scalar_tensor_tensor(gate[:], gate_tanh[:], 1.0, gate_exp[:], ALU.add, ALU.mult)
+
         neg_max = [keep.tile([P, 1], F32, name="neg_max%d" % c) for c in range(TILES)]
+        expd = keep.tile([P, TILES * I], F32, name="expd", tag="val_half1")
+        for c in range(TILES):
+            nc.vector.tensor_reduce(neg_max[c][:], scores[c][:], AX.X, ALU.max, negate=True)
+            nc.scalar.activation(expd[:, cols(c, I)], scores[c][:], ACT.Exp, bias=neg_max[c][:], scale=1.0)
+
+        v_listed0 = keep.tile([P, I], BF16, name="v_listed0")
+        nc.vector.tensor_copy(v_listed0[:], val_pool[0][:].indirect(lists[:]))
+
+        size_rows = bank("size_rows", "size_rows")
+        for t in range(PACK):
+            nc.tensor.transpose(size_rows[:, cols(t, P)], size_col[:, t : t + 1].to_broadcast([P, P]), ident[:])
+
         row_sum = [keep.tile([P, 1], F32, name="row_sum%d" % c) for c in range(TILES)]
         inv_sum = [keep.tile([P, 1], F32, name="inv_sum%d" % c) for c in range(TILES)]
         gated = [keep.tile([P, I], F32, name="gated%d" % c, tag="gated%d" % c, align_bytes=64) for c in range(TILES)]
         w_rows = [keep.tile([P, I], BF16, name="w_rows%d" % c) for c in range(TILES)]
         for c in range(TILES):
-            nc.scalar.activation(v_abs[c][:], block_scores[:, cols(c, G)], ACT.Abs, bias=th_col[:, c : c + 1], scale=-SLOPE)
-            nc.scalar.activation(v_low[c][:], block_scores[:, cols(c, G)], ACT.Relu, bias=th_col[:, c : c + 1], scale=-SLOPE)
-        for c in range(TILES):
-            nc.scalar.activation(v_tanh[c][:], v_abs[c][:], ACT.Tanh, scale=0.5)
-            nc.scalar.activation(v_exp[c][:], v_low[c][:], ACT.Exp, scale=-1.0)
-            nc.vector.scalar_tensor_tensor(gate[c][:], v_tanh[c][:], 1.0, v_exp[c][:], ALU.add, ALU.mult)
-        words = {}
-        for pair in WORD_PAIRS:
-            words[pair] = keep.tile([P, T], F32, name="val_words%d" % pair)
-            for n in range(4):
-                h, part = divmod(n, 4 // 2)
-                width = T // 4
-                nc.scalar.activation(words[pair][:, cols(n, width)].bitcast(BF16).rearrange("p (k f e) -> p k f e", f=2, e=2),
-                                     val_pool[2 * pair + h][:, :, cols(part, width)].rearrange("p f (k e) -> p k f e", e=2), ACT.Copy)
-        expd = keep.tile([P, TILES * I], F32, name="expd", tag="val_raw3")
-        for c in range(TILES):
-            nc.vector.tensor_reduce(neg_max[c][:], scores[c][:], AX.X, ALU.max, negate=True)
-            nc.scalar.activation(expd[:, cols(c, I)], scores[c][:], ACT.Exp, bias=neg_max[c][:], scale=1.0)
-
-        size_rows = bank("size_rows", "size_rows")
-        for t in range(PACK):
-            nc.tensor.transpose(size_rows[:, cols(t, P)], size_col[:, t : t + 1].to_broadcast([P, P]), ident[:])
-        w_grouped = keep.tile([P, PACK * Q], BF16, name="w_grouped", align_bytes=64)
-        w_mx = mx_tiles("w", Q)
-        for c in range(TILES):
             nc.vector.scalar_tensor_tensor(
-                gated[c][:].rearrange("p (g r) -> p g r", r=BLOCK), expd[:, cols(c, I)].rearrange("p (g r) -> p g r", r=BLOCK), 1.0,
-                gate[c][:].unsqueeze(2).to_broadcast([P, G, BLOCK]), ALU.mult, ALU.mult, accum_out=row_sum[c][:])
+                gated[c][:].rearrange("p (g r) -> p g r", r=BLOCK),
+                expd[:, cols(c, I)].rearrange("p (g r) -> p g r", r=BLOCK), 1.0,
+                gate[:, cols(c, G)].unsqueeze(2).to_broadcast([P, G, BLOCK]), ALU.mult, ALU.mult,
+                accum_out=row_sum[c][:])
         for c in range(TILES):
             nc.vector.reciprocal(inv_sum[c][:], row_sum[c][:])
         for c in range(TILES):
@@ -187,43 +182,45 @@ def tile_attend_ownlists_moba_kernel(tc, query, keys, th, size, vals, own, offs,
                     w_rows[c][:, cols(u, 2 * P)].rearrange("p (s e) -> p s e", e=2),
                     gated[c][:].rearrange("p (s t) -> p s t", t=PACK)[:, :, cols(u, 2)], inv_sum[c][:],
                     size_rows[:, cols(u, 2 * P)].rearrange("p (e s) -> p s e", e=2), ALU.mult, ALU.mult)
+        w_grouped = keep.tile([P, PACK * Q], BF16, name="w_grouped", align_bytes=64)
+        w_mx = mx_tiles("w", Q)
         for c in range(TILES):
-            turned = bank(("sums", "sums_back")[c], "w_turned%d" % c)
+            w_turned = bank(("sums", "sums_back")[c], "w_turned%d" % c)
             for u in range(2):
-                nc.tensor.transpose(turned[:, cols(u, P)], w_rows[c][:].bitcast(F32)[:, cols(u, P)], ident[:])
+                nc.tensor.transpose(w_turned[:, cols(u, P)], w_rows[c][:].bitcast(F32)[:, cols(u, P)], ident[:])
             nc.scalar.copy(w_grouped[:, cols(c, PACK * P)].bitcast(F32).rearrange("p (q u) -> p q u", u=2),
-                           turned[:, 0 : 2 * P].rearrange("p (u q) -> p q u", u=2))
+                           w_turned[:, 0 : 2 * P].rearrange("p (u q) -> p q u", u=2))
             quantize(w_mx, w_grouped, cols(c, P))
 
-        v_grouped = keep.tile([P, PACK * E], BF16, name="v_grouped", tag="low1", align_bytes=64)
-        for pair in (1, 0):
-            turned = bank("v_turned%d" % pair, "v_turned%d" % pair)
-            if pair in WORD_PAIRS:
-                listed = keep.tile([P, I], F32, name="v_listed_words%d" % pair)
-                nc.vector.tensor_copy(listed[:], words[pair][:].indirect(lists[:]))
-                for f in range(2):
-                    for u in range(2):
-                        nc.tensor.transpose(turned[:, cols(2 * f + u, P)], listed[:, 2 * u + f : I : 4], ident[:])
-            else:
-                for f in range(2):
-                    listed = keep.tile([P, I], BF16, name="v_listed%d" % (2 * pair + f))
-                    nc.vector.tensor_copy(listed[:], val_pool[2 * pair + f][:].indirect(lists[:]))
-                    for u in range(2):
-                        nc.tensor.transpose(turned[:, cols(2 * f + u, P)], listed[:].bitcast(F32)[:, u : I // 2 : 2], ident[:])
+        v_grouped = keep.tile([P, PACK * E], BF16, name="v_grouped", tag="gate_exp", align_bytes=64)
+        late_listed = keep.tile([P, I + I // 2], F32, name="late_listed", tag="kb_grouped", align_bytes=64)
+        words23 = late_listed[:, 0:I]
+        words1 = late_listed[:, I : I + I // 2]
+
+        def turn_values(pair, sources):
+            v_turned = bank("v_turned%d" % pair, "v_turned%d" % pair)
+            for f in range(2):
+                for u in range(2):
+                    nc.tensor.transpose(v_turned[:, cols(2 * f + u, P)], sources[f][u], ident[:])
             nc.scalar.copy(v_grouped[:, cols(pair, 2 * PACK * P)].bitcast(F32).rearrange("p (f e u) -> p f e u", f=2, u=2),
-                           turned[:].rearrange("p (f u e) -> p f e u", f=2, u=2))
+                           v_turned[:].rearrange("p (f u e) -> p f e u", f=2, u=2))
+
+        nc.vector.tensor_copy(words23, val_words[:].indirect(lists[:]))
+        turn_values(1, [[words23[:, 2 * u + f : I : 4] for u in range(2)] for f in range(2)])
+        nc.vector.tensor_copy(words1.bitcast(BF16), val_pool[1][:].indirect(lists[:]))
+        turn_values(0, [[words[:, u : I // 2 : 2] for u in range(2)] for words in (v_listed0[:].bitcast(F32), words1)])
         v_mx = mx_tiles("v", E, tag="gated0")
         quantize(v_mx, v_grouped, slice(0, E))
 
         result = keep.tile([P, PACK, X], F32, name="result")
-        kept = [keep.tile([P, PACK * P], F32, name="kept%d" % c) for c in range(TILES)]
+        kept = [keep.tile([P, PACK, P], F32, name="kept%d" % c) for c in range(TILES)]
         for c in range(TILES):
             mixed = bank("scores%d" % c, "mixed%d" % c)
             for t in range(PACK):
                 product(mixed[:, cols(t, P)], v_mx, cols(t, P), w_mx, cols(c, P))
-            nc.vector.tensor_tensor(kept[c][:].rearrange("p (t q) -> p t q", t=PACK), mixed[:].rearrange("p (t q) -> p t q", t=PACK),
-                                    own_sb[:].rearrange("p (t q) -> p t q", t=PACK)[:, :, cols(c, P)], ALU.mult)
+            nc.vector.tensor_tensor(kept[c][:], mixed[:].rearrange("p (t q) -> p t q", t=PACK),
+                                    own_sb[:, :, cols(c, P)], ALU.mult)
         for c in range(TILES):
             nc.vector.tensor_reduce(result[:, :, cols(c, X // TILES)],
-                                    kept[c][:].rearrange("p (t x r) -> p t x r", t=PACK, r=Q // X), AX.X, ALU.add)
+                                    kept[c][:].rearrange("p t (x r) -> p t x r", r=Q // X), AX.X, ALU.add)
         nc.sync.dma_start(out.rearrange("(p t) x -> p t x", t=PACK), result[:])

from contextlib import ExitStack

import concourse.mybir as mybir
from concourse.masks import make_identity

D, T, I, Q, X, E, G = 512, 1024, 512, 256, 32, 512, 64
FLOPS = 2 * D * Q * G + 2 * D * Q * I + 2 * I * E * Q

F32 = mybir.dt.float32
BF16 = mybir.dt.bfloat16
U32 = mybir.dt.uint32
U16 = mybir.dt.uint16
U8 = mybir.dt.uint8
FP8X4 = mybir.dt.float8_e4m3fn_x4
ACT = mybir.ActivationFunctionType
ALU = mybir.AluOpType
AX = mybir.AxisListType

P = 128
PACK = 4
BLOCK = I // G
TILES = Q // P
BANK = 512
SLOPE = 14.0 / BLOCK
VECTOR_SLOTS = I // 2
RUN = 4
CAST_PIECES = 2


def cols(n, width):
    return slice(n * width, (n + 1) * width)


def tile_attend_ownlists_moba_kernel(tc, query, keys, th, size, vals, own, offs, out):
    nc = tc.nc
    with ExitStack() as ctx:
        keep = ctx.enter_context(tc.tile_pool(name="keep", bufs=1))
        psum = ctx.enter_context(tc.psum_pool(name="psum", bufs=1))

        def bank(tag, name):
            return psum.tile([P, BANK], F32, tag=tag, name=name)

        def mx_tiles(name, width, tag=""):
            codes = keep.tile([P, width], U32, name=name + "_codes", tag=tag, align_bytes=64)
            scales = keep.tile([P, width], U8, name=name + "_scales", align_bytes=64)
            return codes, scales

        def quantize(operand, grouped, part):
            nc.vector.quantize_mx(out=operand[0][:, part].bitcast(FP8X4), scales=operand[1][:, part],
                                  in_=grouped[:, PACK * part.start : PACK * part.stop])

        def product(dst, left, left_part, right, right_part):
            nc.tensor.matmul_mx(out=dst, lhsT=left[0][:, left_part].bitcast(FP8X4), lhsT_scale=left[1][:, left_part],
                                rhs=right[0][:, right_part].bitcast(FP8X4), rhs_scale=right[1][:, right_part],
                                start=True, stop=True)

        lists = keep.tile([P, I // 16], U16, name="lists")
        key_planes = keys.rearrange("(p t) w -> p t w", t=PACK)
        val_planes = vals.rearrange("(p t) w -> p t w", t=PACK)
        key_pool = [keep.tile([P, T], F32, name="key_pool%d" % t) for t in range(PACK)]
        val_pool = [keep.tile([P, T], F32, name="val_pool%d" % t) for t in range(2)]
        val_half = [keep.tile([P, 2, T // 2], F32, name="val_half%d" % h, tag="val_half%d" % h) for h in range(2)]
        q_raw = keep.tile([P, PACK, Q], F32, name="q_raw")
        th_col = keep.tile([P, TILES], F32, name="th_col")
        size_col = keep.tile([P, PACK], F32, name="size_col")
        own_sb = keep.tile([P, PACK, Q], F32, name="own_sb")

        nc.sync.dma_start(key_pool[0][:], key_planes[:, 0, :])
        nc.sync.dma_start(lists[:], offs)
        for t in range(1, PACK):
            nc.sync.dma_start(key_pool[t][:], key_planes[:, t, :])
        nc.sync.dma_start(q_raw[:], query.rearrange("(p t) q -> p t q", t=PACK))
        nc.sync.dma_start(val_pool[0][:], val_planes[:, 0, :])
        with nc.allow_non_contiguous_dma(reason="one threshold for each partition of a query tile"):
            nc.sync.dma_start(th_col[:], th.rearrange("(c p) o -> p (c o)", p=P))
        nc.sync.dma_start(size_col[:], size.rearrange("o (s t) -> s (o t)", t=PACK))
        for h in range(2):
            nc.sync.dma_start(val_half[h][:], val_planes[:, 2:4, cols(h, T // 2)])
        nc.sync.dma_start(val_pool[1][:], val_planes[:, 1, :])
        nc.sync.dma_start(own_sb[:], own.rearrange("(p t) q -> p t q", t=PACK))

        ident = keep.tile([P, P], F32, name="ident")
        make_identity(nc, ident[:])

        k_listed = keep.tile([P, PACK * I], F32, name="k_listed", tag="k_listed")
        k_grouped = keep.tile([P, PACK * I], BF16, name="k_grouped", align_bytes=64)

        def gather_keys(pair):
            for t in range(2 * pair, 2 * pair + 2):
                nc.vector.tensor_copy(k_listed[:, cols(t, I)], key_pool[t][:].indirect(lists[:]))

        def interleave_keys(copy, pair, slots):
            copy(k_grouped[:].rearrange("p (i t) -> p i t", t=PACK)[:, slots, cols(pair, 2)],
                 k_listed[:, cols(pair, 2 * I)].rearrange("p (f i) -> p i f", f=2)[:, slots, :])

        gather_keys(0)
        interleave_keys(nc.scalar.copy, 0, slice(0, I))
        sums = bank("sums", "sums")
        for r in range(BLOCK):
            nc.tensor.matmul(sums[:, 0:P], lhsT=k_listed[:, r : 2 * I : BLOCK], rhs=ident[:],
                             is_transpose=True, start=(r == 0), stop=(r == BLOCK - 1))
        gather_keys(1)
        interleave_keys(nc.vector.tensor_copy, 1, slice(0, VECTOR_SLOTS))
        interleave_keys(nc.scalar.copy, 1, slice(VECTOR_SLOTS, I))
        kb_grouped = keep.tile([P, PACK * G], BF16, name="kb_grouped", tag="kb_grouped", align_bytes=64)
        kb_places = kb_grouped[:].rearrange("p (g t) -> p g t", t=PACK)
        with nc.allow_low_precision(reason="float32 sums, rounded once on the way to the quantiser"):
            nc.vector.tensor_reduce(kb_places[:, :, 2:4],
                                    k_listed[:, 2 * I : 4 * I].rearrange("p (f g r) -> p g f r", f=2, r=BLOCK),
                                    AX.X, ALU.add)
        k_mx = mx_tiles("k", I)
        quantize(k_mx, k_grouped, slice(0, I))

        q_grouped = keep.tile([P, PACK * Q], BF16, name="q_grouped", align_bytes=64)
        q_mx = mx_tiles("q", Q)
        for c in range(TILES):
            nc.scalar.copy(q_grouped[:, cols(c, PACK * P)].rearrange("p (n i t) -> p n t i", i=RUN, t=PACK),
                           q_raw[:, :, cols(c, P)].rearrange("p t (n i) -> p n t i", i=RUN))
            quantize(q_mx, q_grouped, cols(c, P))
        sums_sb = keep.tile([P, P], F32, name="sums_sb", tag="k_listed")
        nc.scalar.copy(sums_sb[:], sums[:, 0:P])
        sums_back = bank("sums_back", "sums_back")
        nc.tensor.transpose(sums_back[:, 0:P], sums_sb[:], ident[:])
        nc.scalar.copy(kb_places[:, :, 0:2], sums_back[:, 0:P].rearrange("p (f g) -> p g f", f=2))
        kb_mx = mx_tiles("kb", G)
        quantize(kb_mx, kb_grouped, slice(0, G))
        block_scores = bank("block_scores", "block_scores")
        for c in range(TILES):
            product(block_scores[:, cols(c, G)], q_mx, cols(c, P), kb_mx, slice(0, G))
        scores = [bank("scores%d" % c, "scores%d" % c) for c in range(TILES)]
        for c in range(TILES):
            product(scores[c][:], q_mx, cols(c, P), k_mx, slice(0, I))

        val_words = keep.tile([P, T], F32, name="val_words")
        width = T // (2 * CAST_PIECES)
        for h in range(2):
            for piece in range(CAST_PIECES):
                nc.scalar.activation(
                    val_words[:, cols(h * CAST_PIECES + piece, width)].bitcast(BF16).rearrange("p (k f e) -> p k f e", f=2, e=2),
                    val_half[h][:, :, cols(piece, width)].rearrange("p f (k e) -> p k f e", e=2), ACT.Copy)

        gate_in = keep.tile([P, 2, TILES * G], F32, name="gate_in", tag="val_half1")
        gate_exp = keep.tile([P, TILES * G], F32, name="gate_exp", tag="gate_exp", align_bytes=64)
        gate_tanh = keep.tile([P, TILES * G], F32, name="gate_tanh")
        gate = keep.tile([P, TILES * G], F32, name="gate")
        for c in range(TILES):
            for n, func in enumerate((ACT.Abs, ACT.Relu)):
                nc.scalar.activation(gate_in[:, n, cols(c, G)], block_scores[:, cols(c, G)], func,
                                     bias=th_col[:, c : c + 1], scale=-SLOPE)
        nc.scalar.activation(gate_tanh[:], gate_in[:, 0, :], ACT.Tanh, scale=0.5)
        nc.scalar.activation(gate_exp[:], gate_in[:, 1, :], ACT.Exp, scale=-1.0)
        nc.vector.scalar_tensor_tensor(gate[:], gate_tanh[:], 1.0, gate_exp[:], ALU.add, ALU.mult)

        neg_max = [keep.tile([P, 1], F32, name="neg_max%d" % c) for c in range(TILES)]
        expd = keep.tile([P, TILES * I], F32, name="expd", tag="val_half1")
        for c in range(TILES):
            nc.vector.tensor_reduce(neg_max[c][:], scores[c][:], AX.X, ALU.max, negate=True)
            nc.scalar.activation(expd[:, cols(c, I)], scores[c][:], ACT.Exp, bias=neg_max[c][:], scale=1.0)

        v_listed0 = keep.tile([P, I], BF16, name="v_listed0")
        nc.vector.tensor_copy(v_listed0[:], val_pool[0][:].indirect(lists[:]))

        size_rows = bank("size_rows", "size_rows")
        for t in range(PACK):
            nc.tensor.transpose(size_rows[:, cols(t, P)], size_col[:, t : t + 1].to_broadcast([P, P]), ident[:])

        row_sum = [keep.tile([P, 1], F32, name="row_sum%d" % c) for c in range(TILES)]
        inv_sum = [keep.tile([P, 1], F32, name="inv_sum%d" % c) for c in range(TILES)]
        gated = [keep.tile([P, I], F32, name="gated%d" % c, tag="gated%d" % c, align_bytes=64) for c in range(TILES)]
        w_rows = [keep.tile([P, I], BF16, name="w_rows%d" % c) for c in range(TILES)]
        for c in range(TILES):
            nc.vector.scalar_tensor_tensor(
                gated[c][:].rearrange("p (g r) -> p g r", r=BLOCK),
                expd[:, cols(c, I)].rearrange("p (g r) -> p g r", r=BLOCK), 1.0,
                gate[:, cols(c, G)].unsqueeze(2).to_broadcast([P, G, BLOCK]), ALU.mult, ALU.mult,
                accum_out=row_sum[c][:])
        for c in range(TILES):
            nc.vector.reciprocal(inv_sum[c][:], row_sum[c][:])
        for c in range(TILES):
            for u in range(2):
                nc.vector.scalar_tensor_tensor(
                    w_rows[c][:, cols(u, 2 * P)].rearrange("p (s e) -> p s e", e=2),
                    gated[c][:].rearrange("p (s t) -> p s t", t=PACK)[:, :, cols(u, 2)], inv_sum[c][:],
                    size_rows[:, cols(u, 2 * P)].rearrange("p (e s) -> p s e", e=2), ALU.mult, ALU.mult)
        w_grouped = keep.tile([P, PACK * Q], BF16, name="w_grouped", align_bytes=64)
        w_mx = mx_tiles("w", Q)
        for c in range(TILES):
            w_turned = bank(("sums", "sums_back")[c], "w_turned%d" % c)
            for u in range(2):
                nc.tensor.transpose(w_turned[:, cols(u, P)], w_rows[c][:].bitcast(F32)[:, cols(u, P)], ident[:])
            nc.scalar.copy(w_grouped[:, cols(c, PACK * P)].bitcast(F32).rearrange("p (q u) -> p q u", u=2),
                           w_turned[:, 0 : 2 * P].rearrange("p (u q) -> p q u", u=2))
            quantize(w_mx, w_grouped, cols(c, P))

        v_grouped = keep.tile([P, PACK * E], BF16, name="v_grouped", tag="gate_exp", align_bytes=64)
        late_listed = keep.tile([P, I + I // 2], F32, name="late_listed", tag="kb_grouped", align_bytes=64)
        words23 = late_listed[:, 0:I]
        words1 = late_listed[:, I : I + I // 2]

        def turn_values(pair, sources):
            v_turned = bank("v_turned%d" % pair, "v_turned%d" % pair)
            for f in range(2):
                for u in range(2):
                    nc.tensor.transpose(v_turned[:, cols(2 * f + u, P)], sources[f][u], ident[:])
            nc.scalar.copy(v_grouped[:, cols(pair, 2 * PACK * P)].bitcast(F32).rearrange("p (f e u) -> p f e u", f=2, u=2),
                           v_turned[:].rearrange("p (f u e) -> p f e u", f=2, u=2))

        nc.vector.tensor_copy(words23, val_words[:].indirect(lists[:]))
        turn_values(1, [[words23[:, 2 * u + f : I : 4] for u in range(2)] for f in range(2)])
        nc.vector.tensor_copy(words1.bitcast(BF16), val_pool[1][:].indirect(lists[:]))
        turn_values(0, [[words[:, u : I // 2 : 2] for u in range(2)] for words in (v_listed0[:].bitcast(F32), words1)])
        v_mx = mx_tiles("v", E, tag="gated0")
        quantize(v_mx, v_grouped, slice(0, E))

        result = keep.tile([P, PACK, X], F32, name="result")
        kept = [keep.tile([P, PACK, P], F32, name="kept%d" % c) for c in range(TILES)]
        for c in range(TILES):
            mixed = bank("scores%d" % c, "mixed%d" % c)
            for t in range(PACK):
                product(mixed[:, cols(t, P)], v_mx, cols(t, P), w_mx, cols(c, P))
            nc.vector.tensor_tensor(kept[c][:], mixed[:].rearrange("p (t q) -> p t q", t=PACK),
                                    own_sb[:, :, cols(c, P)], ALU.mult)
        for c in range(TILES):
            nc.vector.tensor_reduce(result[:, :, cols(c, X // TILES)],
                                    kept[c][:].rearrange("p t (x r) -> p t x r", r=Q // X), AX.X, ALU.add)
        nc.sync.dma_start(out.rearrange("(p t) x -> p t x", t=PACK), result[:])
